import numpy as np, ml_dtypes
CORES = [1,5,17,21,33,37,49,53]
N = 8
BF = ml_dtypes.bfloat16
V, S, P, SH, RO = 512, 6, 4, 3, 5
M, K1, K2, K3, K4, K5 = 4096, 1597, 613, 911, 1223, 74
def pack(s, li):
    return {"x": np.ascontiguousarray(s.reshape(N, 128, V)).astype(np.float32).astype(BF), "liar": np.ascontiguousarray(li).astype(np.int32)}
def states(rng):
    mid = rng.integers(30, 226, (N, 8, 16, 1)); wid = rng.integers(15, 90, (N, 8, 1, 1))
    return np.clip(np.rint(mid + wid * rng.standard_normal((N, 8, 16, V))), 0, 255).astype(np.int64)
def lies(rng, s, li):
    kind = rng.integers(0, 3, (N, 8, 1, V))
    w = np.where(kind == 0, 255 * rng.integers(0, 2, s.shape), np.where(kind == 1, 255 * rng.integers(0, 2, (N, 8, 1, V)), rng.integers(0, 256, s.shape)))
    return np.where(li[:, :, None, :], w, s)
def hit(u):
    return ((u * u >> 7) + u) & (M - 1)
def draws(i, c, t):
    m = np.arange(S, dtype=np.int64)[:, None]
    return hit((i * K1 + c * (K2 + K5 * m) + t * K3 + m * K4) & (M - 1))
def comps(rng, c):
    r = np.clip(np.rint(c[:, None, :] * 0.0625 + 50 * rng.standard_normal((8, 16, M))), 0, 255).astype(np.int64)
    left = c - np.add.reduce(r, axis=1)
    for i in rng.permutation(16):
        a = np.clip(left, -r[:, i], 255 - r[:, i]); r[:, i] += a; left = left - a
    return r
def steered(rng, us, m):
    c = np.full(M, M, np.int64); back = pow(K2 + K5 * m, 1023, M)
    for k in range(12):
        w = us[rng.integers(0, len(us), M)]
        c = np.where(c > 4080, ((w - np.arange(M, dtype=np.int64) * K1 - m * K4) * back) & (M - 1), c)
    return np.minimum(c, 4080)
def placed(u, d):
    c = (((d - K4) >> 1) * pow(K5 >> 1, 1023, 2048)) & 2047
    c = np.concatenate([c, c + 2048]); u = np.concatenate([u, u]); k = c <= 4080; c = c[k]; u = u[k]
    return ((u - c * K2) * pow(K1, 1023, M)) & (M - 1), c
def thrice():
    u = np.arange(M, dtype=np.int64); h = hit(u).astype(np.int16); us, ds = [], []
    for a in range(0, M // 2, 128):
        d = 2 * np.arange(a, a + 128, dtype=np.int64)[:, None] + 1; n = np.zeros((128, M), np.int8)
        for k in range(1, min(S, 8)): n += (h[(u + k * d) & (M - 1)] == h)
        j, i = np.nonzero(n >= 2); us.append(u[i]); ds.append(d[j, 0])
    return np.concatenate(us), np.concatenate(ds)
def twice():
    u = np.arange(M, dtype=np.int64); h = hit(u); n = np.zeros((M, M), np.int8)
    for m in range(S): n[h, ((u - h * K1 - m * K4) * pow(K2 + K5 * m, 1023, M)) & (M - 1)] += 1
    return np.nonzero(n[:, :4081] >= 2)
def some(rng, a):
    e = rng.permutation(len(a[0]))[:48]
    return a[0][e], a[1][e]
def setup_inputs(rng):
    s = states(rng); li = rng.random((N, 8, V)) < rng.choice(np.array([0.03, 0.1, 0.2, 0.35]), (N, 8, 1))
    return pack(lies(rng, s, li), li)
def setup_inputs_alike(rng):
    s = states(rng); li = rng.random((N, 8, V)) < 0.1; o = rng.permutation(8)
    for g in (o[0], o[1]): li[:, g] = False
    s = lies(rng, s, li)
    s[:, o[0]] = rng.integers(0, 256, (16, 1))
    s[:, o[1]] = rng.integers(0, 255, (16, 1)) + rng.integers(0, 2, (N, 16, V))
    s[:, o[2]] = 255 * rng.integers(0, 2, (N, 16, V))
    a = rng.integers(0, 256, (2, 16, 1)); s[:, o[3]] = np.where(rng.random((N, 1, V)) < 0.5, a[0], a[1])
    s[:, o[4]] = np.where(li[:, o[4]][:, None, :], s[:, o[4]], rng.integers(0, 256, (16, 1)))
    return pack(s, li)
def setup_inputs_ends(rng):
    s = states(rng); li = rng.random((N, 8, V)) < 0.1; s = lies(rng, s, li)
    k = rng.integers(0, 8, (N, 8, 1, V)); s = np.where(k == 0, 0, np.where(k == 1, 255, s))
    s[:, ::2, :, 0] = 255; s[:, 1::2, :, 0] = 0; s[:, ::2, :, V - 1] = 0; s[:, 1::2, :, V - 1] = 255
    li[0, :, 0] = True; li[N - 1, :, V - 1] = True; li[0, :, V - 1] = False; li[N - 1, :, 0] = False
    return pack(s, li)
def setup_inputs_liars(rng):
    s = states(rng); li = rng.random((N, 8, V)) < 0.25; o = rng.permutation(8)
    li[:, o[0]] = False; li[:, o[1]] = True
    i = int(rng.integers(0, M)); li[:, o[2]] = True; li[i // V, o[2], i % V] = False
    li[:, o[3]] = False; li[rng.integers(0, N), o[3], rng.integers(0, V)] = True
    li[:, o[4]] = False; li[rng.integers(0, N), o[4]] = True
    li[:, o[5]] = False; li[:, o[5], ::2] = True
    li[:, o[6]] = False; li[:, o[6], V // 4:V // 2] = True
    s = lies(rng, s, li)
    b = rng.integers(0, 256, 16); s[i // V, o[2], :, i % V] = b
    for p in draws(np.array([i]), np.array([int(np.sum(b))]), 0)[:, 0]: s[int(p) // V, o[2], :, int(p) % V] = b
    return pack(s, li)
def setup_inputs_steer(rng):
    o = rng.permutation(8); h = hit(np.arange(M, dtype=np.int64)); q = rng.permutation(N)
    c = rng.integers(0, 4081, (8, M)); li = rng.random((8, M)) < 0.1; li[o[0]] = False
    top = np.flatnonzero(np.bincount(h, minlength=M) >= 4)
    for g, m in ((o[0], 0), (o[1], S - 1), (o[2], int(rng.integers(0, S)))): c[g] = steered(rng, np.flatnonzero(h == rng.choice(top)), m)
    for g, w in ((o[3], q[0]), (o[4], q[1])): c[g] = steered(rng, np.flatnonzero(h // V == w), int(rng.integers(0, S)))
    self2 = twice(); three = placed(*thrice()); close = placed(np.arange(4, dtype=np.int64), np.ones(4, np.int64))
    for j in range(3):
        g = o[5 + j]; li[g] = rng.random(M) < 0.5
        a = [some(rng, close), some(rng, self2), some(rng, three)]
        for i, k in a[1:]:
            p = draws(i, k, 0); c[g, p] = rng.integers(0, 300, p.shape)
        p = draws(a[2][0], a[2][1], 0)[0]; c[g, p] = rng.integers(3600, 4081, p.shape)
        for i, k in a[j + 1:] + a[:j + 1]:
            c[g, i] = k; li[g, i] = False
    s = comps(rng, c)
    return pack(np.ascontiguousarray(s.reshape(8, 16, N, V).transpose(2, 0, 1, 3)), li.reshape(8, N, V).transpose(1, 0, 2))
def setup_inputs_spread(rng):
    s = np.floor(np.exp2(8 * rng.random((N, 8, 1, V))) * rng.random((N, 8, 16, V))).astype(np.int64)
    s = np.clip(np.where(rng.random((N, 8, 1, 1)) < 0.4, 255 - s, s), 0, 255)
    li = rng.random((N, 8, V)) < 0.5 * rng.random((N, 8, 1))
    q = rng.permutation(N); li[q[0]] = False; li[q[1]] = True
    return pack(s, li)
def check_inputs(d):
    bad = []
    v = d["x"].astype(np.float32)
    if not np.all((v >= 0) & (v <= 255) & (v == np.floor(v))): bad.append("range of x")
    if np.min(d["liar"]) < 0 or np.max(d["liar"]) > 1: bad.append("range of liar")
    return bad
def reference(x, liar):
    s = np.ascontiguousarray(x.astype(np.float32).astype(np.int32).reshape(N, 8, 16, V).transpose(1, 2, 0, 3)).reshape(8, 16, M)
    stay = np.ascontiguousarray(liar.transpose(1, 0, 2)).reshape(8, 1, M) == 1
    ids = np.arange(M, dtype=np.int64)
    for t in range(RO):
        c = np.add.reduce(s.astype(np.int64), axis=1)
        tot, hi, lo = 0, 0, 255
        for m in range(S):
            u = (ids * K1 + c * (K2 + K5 * m) + t * K3 + m * K4) & (M - 1)
            peer = ((u * u >> 7) + u) & (M - 1)
            v = np.take_along_axis(s, peer[:, None, :], 2)
            tot = tot + v; hi = np.maximum(hi, v); lo = np.minimum(lo, v)
        s = np.where(stay, s, (tot - hi - lo + P * s) >> SH)
    y = np.ascontiguousarray(s.reshape(8, 16, N, V).transpose(2, 0, 1, 3)).reshape(N, 128, V)
    return {"y": y.astype(np.float32).astype(BF)}

from concourse.bass import DstId, RemoteDMATransfer
from concourse.mybir import AluOpType as ALU, ActivationFunctionType as ACT

NR = 8
RO = 5
ZC = 4096
TW = 4112
MAGIC = 12582912.0
NRB = 4
MAXCH = 2

CFG = {
    "chunks": [[2, 2, 2, 1, 1]] * 5,
    "gath": [[1] * 8] * 5,
    "batch": [[4, 4]] + [[6, 2]] * 4,
}

PERIOD = 835
PLAN = """
s ax3:-1029x ax2:-1029x ax6:-1029x al1:-1029x ax1:-1029x ax5:-1029x ax4:-1029x ax7:-1029x Ec1:-1029g ls1:-1029a
s xs1:-1029s z2:-700v so1:-1019s dma1:-1018v KC1:-1013g Y1:-985g dmb1:-966v jx1:-954v dn1:-945a PH1:-937g J1:-896g
s R1:-887v kx1:-876v R3:-864v lo1:-1028a A5:-846a jy1:-842v sl1:-830g A1:-827a k8f1:-823v voff1:-810v A6:-808a
s j16p1:-806v D1:-792v A4:-788a H1:-778v sxa1:-771g A8:-769a ta1:-760v Dv1:-743a ml1:-737v R5:-729v Da1:-727a
s sxb1:-712g bc1:-705v A7:-705a z1:-701v A2:-686a R4:-683v R8:-671v A3:-666a Dm1:-660v C1:-653g R7:-639v Ar1:-639a
s mh1:-627v KS1:-616v tb1:-598v Q1:-574g kt1:-570v li1:-560s R6:-545v base3:-530a R2:-528v kt3:-523v rep1:-514p
s kt4:-498v base2:-491a kt2:-473v rep2:-470p base1:-466a ev1:-448v km1:-439p ev2:-420a rep4:-404p rep3:-403p
s xs2:-392v lb1:-361v ev4:-357a xu1:-350v lsm1:-341p ev3:-335v km2:-332p lse1:-300a xa1:-279v rep5:-277p xq1:-256v
s rep7:-248p xs3:-241v ev5:-239a bl1:-227v ltm1:-219p rep6:-184p xu2:-183v ev7:-181a xp1:-169v rep8:-155p xl1:-140v
s xa2:-139v ev6:-124a ix1:-114v Hh1:-105v xq2:-102v bl2:-76v ev8:-66a xp2:-32v blb1:-18v xl2:64v P1:165v ix2:177v
s lt1:191v N1:195a blb2:327v
m ga2:0a ga1:44v ga4:66a mx1:92v e1_1:129p ga3:132a e2_1:148p e3_1:162p mn1:181v ga6:197a ga5:204a mx2:206v
m e1_2:219p fl1:250v rep2:276p mn2:279v e2_2:286p e3_2:331p mx3:338v rep1:340p e1_3:369p mn3:377v ga7:407a fl2:417v
m ga8:418a e2_3:429p e3_3:433p mx4:442v e1_4:451p rep4:465p fl3:466v ev2:474a ev1:484v km1:509p ev4:529a mn4:540v
m rep3:564p mn5:564v ev3:577a xs1:582v e2_4:582p e3_4:589p mx5:608v rep5:613p e1_5:624p ev5:626a xu1:632v fl4:651v
m e2_5:653p e3_5:659p xa1:662v rep7:671p fl5:682v xq1:693v rep8:702p ev7:712a xp1:718v rep6:730p ev8:741v km2:760p
m ev6:769a ix1:787v xs2:900v xu2:912v xa2:946v xq2:1029v xp2:1103v ix2:1157v
l ga4:0a ga3:0v ga1:66a e1_2:75p mx2:96v ga2:132a e2_2:148p mn2:151v ga6:182a mx1:206v e1_1:212p e3_2:216p mn1:246v
l ga5:263a e2_1:267p fl2:278v e3_1:302p fl1:341v ga7:342a mx3:351v sy1:360g mn3:394v ga8:408a e2_3:415p sy2:419g
l mx4:438v e1_3:445p e2_4:445p e3_3:447p e1_4:456p fl3:465v sy3:492g mn4:505v e3_4:507p e1_5:522p fl4:531v mx5:543v
l ayo1:551x sy4:552g mn5:567v e2_5:576p e3_5:600p ayp1:611x fl5:615v yo1:627a yn1:820a yf1:820s
"""

SCRATCH = {
    "Xs": ("dram", [8, 128, 64], "bfloat16"), "Ls": ("dram", [8, 128, 4], "int32"),
    "Dl": ("dram", [8, 128, 4], "int32"), "Dy": ("dram", [8, 128, 64], "bfloat16"),
    "TB0": ("sbuf", [128, TW], "bfloat16"), "TB1": ("sbuf", [128, TW], "bfloat16"),
    "G": ("sbuf", [128, 3072], "bfloat16"), "MX": ("sbuf", [128, 3072], "bfloat16"),
    "MN": ("sbuf", [128, 3072], "bfloat16"),
    "DM": ("sbuf", [128, 384 * MAXCH], "bfloat16"), "DN": ("sbuf", [128, 384 * MAXCH], "bfloat16"),
    "P8": ("sbuf", [128, 128], "bfloat16"), "N8": ("sbuf", [128, 128], "bfloat16"),
    "H": ("sbuf", [128, 128], "bfloat16"), "H16": ("sbuf", [128, 128], "float16"),
    "R": ("sbuf", [128, 1024], "bfloat16"), "A": ("sbuf", [128, 1024], "bfloat16"),
    "KS": ("sbuf", [128, 160], "float16"), "KT": ("sbuf", [128, 512], "float16"),
    "E3": ("sbuf", [128, 4], "int32"), "KC": ("sbuf", [128, 64], "float32"),
    "Y": ("sbuf", [128, 160], "float32"), "PH": ("sbuf", [128, 128], "bfloat16"),
    "J8": ("sbuf", [128, 128], "bfloat16"), "Q": ("sbuf", [128, 128], "bfloat16"),
    "C0": ("sbuf", [128, 320], "float32"), "BASE": ("sbuf", [128, 960], "float32"),
    "ti": ("sbuf", [128, 8], "int32"), "tf": ("sbuf", [128, 16], "float32"),
    "Dd": ("sbuf", [128, 160], "float32"), "Da": ("sbuf", [128, 160], "float32"),
    "Dv": ("sbuf", [128, 160], "float32"), "MH": ("sbuf", [128, 256], "float16"),
    "Li": ("sbuf", [128, 64], "int32"), "Lb": ("sbuf", [128, 64], "bfloat16"),
    "lS": ("sbuf", [128, 512], "bfloat16"), "bl": ("sbuf", [128, 512], "float16"),
    "LT": ("sbuf", [128, 192], "bfloat16"),
    "xs": ("sbuf", [128, 192], "int32"), "xu": ("sbuf", [128, 192], "int32"), "xq": ("sbuf", [128, 192], "int32"),
    "xp": ("sbuf", [128, 192], "int32"), "IDX": ("sbuf", [128, 192], "uint16"),
    "E0": ("psum", [128, 512], "float32"), "E1": ("psum", [128, 512], "float32"),
    "IX": ("psum", [128, 512], "float32"), "W": ("psum", [128, 512], "float32"),
}
for _t in range(RO + 1):
    SCRATCH["S%d" % _t] = ("sbuf", [128, 512], "bfloat16")
for _b in range(NRB):
    SCRATCH["B%d" % _b] = ("psum", [128, 512], "float32")
PSUM = [n for n in SCRATCH if SCRATCH[n][0] == "psum"]

SEMAPHORES = (["c_p", "c_v", "c_a", "c_g", "dx", "dl", "dlo", "dso", "dli", "al", "ayo", "ayp", "loc",
               "dy0", "dy1", "dy2"] + ["ax%d" % k for k in range(7)])

KW = [(0, 0), (0, 1), (0, 2), (1, 2), (1, 3), (1, 4), (1, 5), (2, 5), (2, 6), (2, 7)]
CUT = {-12: (0, 0), -14: (1, 0), 4: (2, 1), 2: (3, 1)}


def order_of(T, topo, r):
    for a in (1, -1):
        if topo.chip(T.cores[(r - a) % NR]) == topo.chip(T.cores[r]):
            return a, [(r + a * (p + 1)) % NR for p in range(NR)]
    return 1, [(r + p + 1) % NR for p in range(NR)]


def bits(es):
    m = 0
    for e in es:
        m |= 1 << e
    return m


def spans(sizes):
    out, p = [], 0
    for s in sizes:
        out.append((p, p + s))
        p += s
    return out


def build(g, core, T, topo, cfg):
    r = T.rank_of(core)
    a_r, o = order_of(T, topo, r)
    pos_at = [order_of(T, topo, d)[1].index(r) for d in range(NR)]
    near = o[6]
    e_far = topo.engines(core, T.cores[o[0]])
    e_near = [e for e in topo.engines(core, T.cores[near]) if e not in e_far]
    sem = T.sem
    ops, hist, loc, ph, cnt = [], {}, [0], [-1], {}

    def add(name, engs, cyc, rd, wr, emit, n=1, kind="c", s=None, val=0, gn=0, after=()):
        me = len(ops)
        deps = {}
        for d in after:
            deps[d] = False
        acc = [(b, lo, hi, False) for b, lo, hi in rd] + [(b, lo, hi, True) for b, lo, hi in wr]
        for b, lo, hi, w in acc:
            ps = b in PSUM
            if ps:
                lo, hi, w = 0, 512, True
            for (l2, h2, op2, w2) in hist.get(b, []):
                if op2 != me and l2 < hi and lo < h2 and (w or w2):
                    deps[op2] = deps.get(op2, False) or not ps
        for b, lo, hi, w in acc:
            if b in PSUM:
                lo, hi, w = 0, 512, True
            h = hist.setdefault(b, [])
            if w:
                h[:] = [x for x in h if not (lo <= x[0] and x[1] <= hi)]
            h.append((lo, hi, me, w))
        nm = name.rstrip("0123456789")
        cnt[(ph[0], nm)] = cnt.get((ph[0], nm), 0) + 1
        ops.append({"ph": ph[0], "key": nm + str(cnt[(ph[0], nm)]), "name": name, "engs": engs, "cyc": cyc,
                    "emit": emit, "n": n, "kind": kind, "sem": s, "val": val, "gn": gn, "deps": deps})
        return me

    def V(name, cyc, rd, wr, emit):
        return add(name, "v", {"v": cyc}, rd, wr, lambda q, e: [emit(q)])

    def ts(name, out, in0, s1, s2, op0, op1, cyc, rd, wr):
        if op1 is None:
            return V(name, cyc, rd, wr, lambda q: q.tensor_scalar(out, in0, s1, None, op0))
        return V(name, cyc, rd, wr, lambda q: q.tensor_scalar(out, in0, s1, s2, op0, op1))

    def tt(name, out, in0, in1, op, cyc, rd, wr):
        return V(name, cyc, rd, wr, lambda q: q.tensor_tensor(out, in0, in1, op))

    def cp(name, out, in_, cyc, rd, wr, gn=0):
        def emit(q, e):
            return [q.tensor_copy(out, in_)] if e == "v" else [q.activation(out, in_, ACT.Copy)]
        return add(name, "va", {"v": cyc, "a": cyc}, rd, wr, emit, gn=gn)

    def act(name, out, in_, func, bias, scale, cyc, rd, wr):
        return add(name, "a", {"a": cyc}, rd, wr, lambda q, e: [q.activation(out, in_, func, bias=bias, scale=scale)])

    def mm(name, lst, rd, wr):
        cyc = sum(max(64, x[5]) for x in lst)
        return add(name, "p", {"p": cyc}, rd, wr,
                   lambda q, e: [q.matmul(x[0], x[1], x[2], x[3], x[4]) for x in lst], n=len(lst))

    gl = []

    def G(name, ns, rd, wr, emit, kind="c"):
        me = add(name, "g", {"g": ns}, rd, wr, lambda q, e: [emit(q)], kind=kind, after=gl[-1:])
        gl.append(me)
        return me

    def iota(name, buf, n, pat, base, ch, small=True):
        ap = T[buf][:, 0:n]
        if small:
            return G(name, 130 + 1.66 * n, [], [(buf, 0, n)],
                     lambda q: q.iota(ap, pat, base, ch, allow_small_or_imprecise_dtypes=True))
        return G(name, 130 + 1.66 * n, [], [(buf, 0, n)], lambda q: q.iota(ap, pat, base, ch))

    def dmas(name, eng, s, lst, rd, wr):
        return add(name, eng, {eng: 0.0}, rd, wr, lambda q, e: [q.dma_start(x[0], x[1]) for x in lst], n=len(lst),
                   kind="d", s=s)

    def dma(name, eng, s, out, in_, rd, wr):
        return dmas(name, eng, s, [(out, in_)], rd, wr)

    def ext(name, s, val, t, wr, after=()):
        return add(name, "x", {"x": t}, [], wr, None, kind="x", s=s, val=val, after=after)

    def send(name, items, rd):
        trs = []
        for d, es, s, src, dst in items:
            rid, pid, _ = topo.addr(T.cores[d])
            trs.append(RemoteDMATransfer(dst_ids=[DstId(rid=rid, pnc=pid)], dma_engine_mask=bits(es),
                                         remote_sem=sem[s], src=src, dst=dst))
            loc[0] += len(es)
        return G(name, 500, rd, [], lambda q: q.remote_dma_fused(trs, local_sem=sem["loc"]), kind="r")

    S = [T["S%d" % t] for t in range(RO + 1)]
    TB = [T.TB0, T.TB1]

    dma("xs", "s", "dx", T.Xs[:], T.x[:], [], [("Xs", 0, 1)])
    dma("ls", "a", "dl", T.Ls[:], T.liar[:], [], [("Ls", 0, 1)])
    dma("lo", "a", "dlo", T.Dl[7], T.liar[r], [], [("Dl", 7, 8)])
    dma("so", "s", "dso", S[0][:, 448:512], T.x[16 * r:16 * r + 16, :], [], [("S0", 448, 512)])

    iota("Ec", "E3", 3, [[16, 3]], 0, 1, small=False)
    iota("KC", "KC", 64, [[-1, 64]], 0, 1)
    iota("Y", "Y", 160, [[1, 160]], -16, 0)
    iota("PH", "PH", 128, [[0, 8], [1, 16]], 0, 0)
    iota("J8", "J8", 128, [[0, 16], [1, 8]], 0, 0)

    others = [d for d in range(NR) if d != r]
    far = [d for d in others if d != near]
    send("sl", [(d, [e_far[k]], "al", T.Ls[d], T.Dl[pos_at[d]]) for k, d in enumerate(far)]
         + [(near, e_near[0:1], "al", T.Ls[near], T.Dl[pos_at[near]])], [("Ls", 0, 1)])
    first = [d for d in far if pos_at[d] < 4]
    second = [d for d in far if pos_at[d] >= 4]
    na, nb = len(e_far) // len(first), len(e_far) // len(second)

    def xitem(d, es):
        p = pos_at[d]
        return (d, es, "ax%d" % p, T.Xs[d], S[0][:, 64 * p:64 * p + 64])
    send("sxa", [xitem(d, e_far[na * k:na * k + na]) for k, d in enumerate(first)] + [xitem(near, e_near[0:2])],
         [("Xs", 0, 1)])
    send("sxb", [xitem(d, e_far[nb * k:nb * k + nb]) for k, d in enumerate(second)], [("Xs", 0, 1)])
    iota("C0", "C0", 320, [[911, 5], [(2560 * a_r) % 4096, 8], [488, 8]], (2560 * (r + a_r)) % 4096, 0)
    iota("Q", "Q", 128, [[1, 16], [16, 8]], 0, 0)

    ext("al", "al", 7, 4600, [("Dl", 0, 7)])
    for p in range(7):
        ext("ax%d" % p, "ax%d" % p, na if p < 4 else (nb if p < 6 else 2), 5800 if p < 4 else (6800 if p < 6 else 5500),
            [("S0", 64 * p, 64 * p + 64)])
    dma("li", "s", "dli", T.Li[0:64, :], T.Dl[:], [("Dl", 0, 8)], [("Li", 0, 64)])

    nch = 384 * MAXCH
    V("dma", nch / 2, [], [("DM", 0, nch)], lambda q: q.memset(T.DM[:], 1.0))
    V("dmb", 64, [], [("DM", 0, nch)], lambda q: q.memset(T.DM[:, 0:nch:6], 0.0))
    act("dn", T.DN[:], T.DM[:], ACT.Identity, 256.0, -256.0, nch, [("DM", 0, nch)], [("DN", 0, nch)])
    for k in range(2):
        V("z%d" % k, 64, [], [("TB%d" % k, ZC, TW)], lambda q, k=k: q.memset(TB[k][:, ZC:TW], 0.0))
    kcol = T.KC[:, 0:1]
    ti, tf = T.ti, T.tf
    ts("kx", ti[:, 0:1], T.E3[:, 0:1], 7, None, ALU.bitwise_and, None, 64, [("E3", 0, 3)], [("ti", 0, 1)])
    ts("k8f", tf[:, 0:1], ti[:, 0:1], 16.0, 2.5, ALU.mult, ALU.add, 64, [("ti", 0, 1)], [("tf", 0, 1)])
    ts("D", T.Dd[:], T.Y[:], tf[:, 0:1], None, ALU.subtract, None, 160, [("Y", 0, 160), ("tf", 0, 1)], [("Dd", 0, 160)])
    act("Da", T.Da[:], T.Dd[:], ACT.Abs, 0.0, 1.0, 160, [("Dd", 0, 160)], [("Da", 0, 160)])
    act("Dv", T.Dv[:], T.Dd[:], ACT.Identity, 798.0, 74.0, 160, [("Dd", 0, 160)], [("Dv", 0, 160)])
    ts("Dm", T.Da[:], T.Da[:], 3.0, None, ALU.is_lt, None, 160, [("Da", 0, 160)], [("Da", 0, 160)])
    tt("KS", T.KS[:], T.Dv[:], T.Da[:], ALU.mult, 320, [("Dv", 0, 160), ("Da", 0, 160)], [("KS", 0, 160)])
    ts("mh", T.MH[:, 0:128], T.PH[:], 8.0, None, ALU.is_ge, None, 64, [("PH", 0, 128)], [("MH", 0, 128)])
    ts("ml", T.MH[:, 128:256], T.PH[:], 8.0, None, ALU.is_lt, None, 64, [("PH", 0, 128)], [("MH", 128, 256)])
    for off, (slot, half) in CUT.items():
        tt("kt", T.KT[:, 128 * slot:128 * slot + 128], T.KS[:, 16 + off:144 + off], T.MH[:, 128 * half:128 * half + 128],
           ALU.mult, 200, [("KS", 0, 160), ("MH", 128 * half, 128 * half + 128)], [("KT", 128 * slot, 128 * slot + 128)])
    for j in range(8):
        ts("R", T.R[:, 128 * j:128 * j + 128], T.PH[:], 8.0, T.KC[:, j:j + 1], ALU.mult, ALU.is_equal, 64,
           [("PH", 0, 128), ("KC", 0, 64)], [("R", 128 * j, 128 * j + 128)])
    for p in range(8):
        act("A", T.A[0:64, 128 * p:128 * p + 128], T.J8[0:64, :], ACT.Abs, T.KC[0:64, 8 * p:8 * p + 1], -1.0, 128,
            [("J8", 0, 128), ("KC", 0, 64)], [("A", 128 * p, 128 * p + 128)])
    act("Ar", T.A[0:64, :], T.A[0:64, :], ACT.Relu, 1.0, -1.0, 1024, [("A", 0, 1024)], [("A", 0, 1024)])
    ts("H", T.H[:], T.Y[:, 16:144], kcol, 0.5, ALU.is_equal, ALU.mult, 128, [("Y", 0, 160), ("KC", 0, 64)], [("H", 0, 128)])
    ts("Hh", T.H16[:], T.H[:], 1.0, None, ALU.mult, None, 64, [("H", 0, 128)], [("H16", 0, 128)])
    ts("P8", T.P8[:], T.Q[:], kcol, 0.125, ALU.is_equal, ALU.mult, 64, [("Q", 0, 128), ("KC", 0, 64)], [("P8", 0, 128)])
    act("N8", T.N8[:], T.P8[:], ACT.Identity, 0.0, -1.0, 128, [("P8", 0, 128)], [("N8", 0, 128)])
    ts("jx", ti[:, 1:2], T.E3[:, 0:1], 112, None, ALU.bitwise_and, None, 64, [("E3", 0, 3)], [("ti", 1, 2)])
    ts("j16p", tf[:, 1:2], ti[:, 1:2], 2.5, None, ALU.add, None, 64, [("ti", 1, 2)], [("tf", 1, 2)])
    ts("jy", tf[:, 2:3], ti[:, 1:2], 979.0, None, ALU.mult, None, 64, [("ti", 1, 2)], [("tf", 2, 3)])
    ts("voff", ti[:, 4:7], T.E3[:, 0:3], tf[:, 1:2], 1.0 / 6.0, ALU.subtract, ALU.mult, 64,
       [("E3", 0, 3), ("tf", 1, 2)], [("ti", 4, 7)])
    ts("ta", tf[:, 4:7], T.E3[:, 0:3], 1223.0, tf[:, 2:3], ALU.mult, ALU.subtract, 64,
       [("E3", 0, 3), ("tf", 2, 3)], [("tf", 4, 7)])
    ts("tb", tf[:, 8:11], ti[:, 4:7], 2451.0, None, ALU.mult, None, 64, [("ti", 4, 7)], [("tf", 8, 11)])
    tt("bc", tf[:, 12:15], tf[:, 4:7], tf[:, 8:11], ALU.add, 64, [("tf", 4, 11)], [("tf", 12, 15)])
    for rr in range(3):
        act("base", T.BASE[:, rr:960:3], T.C0[:], ACT.Identity, tf[:, 12 + rr:13 + rr], 1.0, 320,
            [("C0", 0, 320), ("tf", 12, 15)], [("BASE%d" % rr, 0, 1)])
    base_rd = [("BASE%d" % rr, 0, 1) for rr in range(3)]

    def kweight(rr, vo):
        off = 16 * rr - 6 * vo
        if off in CUT:
            s = CUT[off][0]
            return T.KT[:, 128 * s:128 * s + 128]
        return T.KS[:, 16 + off:144 + off]
    k_rd = [("KS", 0, 160), ("KT", 0, 512)]

    def kmm(name, src, sname, p0, p1, flag, pb="IX"):
        n = 8 * (p1 - p0)
        lst = []
        for rr in range(3):
            out = T[pb][:, rr:3 * n:3]
            mine = [vo for (q2, vo) in KW if q2 == rr]
            if flag:
                lst.append((out, T.H[:], T.LT[:, 24 * p0 + rr:24 * p1:3], True, False, n))
            for k, vo in enumerate(mine):
                lst.append((out, kweight(rr, vo), src[:, 64 * p0 + vo:64 * p1:8], (not flag) and k == 0,
                            k == len(mine) - 1, n))
        rd = k_rd + [(sname, 64 * p0, 64 * p1)]
        if flag:
            rd = rd + [("H", 0, 128), ("LT", 24 * p0, 24 * p1)]
        mm(name, lst, rd, [(pb, 0, 1)])

    V("lb", 64, [("Li", 0, 64)], [("Lb", 0, 64)], lambda q: q.tensor_copy(T.Lb[0:64, :], T.Li[0:64, :]))
    bank = [0]

    def next_bank():
        b = "B%d" % (bank[0] % NRB)
        bank[0] += 1
        return b
    mm("lsm", [(T.E0[:, 64 * p:64 * p + 64], T.A[0:64, 128 * p:128 * p + 128], T.Lb[0:64, :], True, True, 64)
               for p in range(8)], [("A", 0, 1024), ("Lb", 0, 64)], [("E0", 0, 1)])
    cp("lse", T.lS[:], T.E0[:], 512, [("E0", 0, 1)], [("lS", 0, 512)])
    kmm("ltm", T.lS, "lS", 0, 8, False, "E1")

    def offsets(t, p0, p1):
        c0, c1 = 24 * p0, 24 * p1
        n = c1 - c0
        kmm("km", S[t], "S%d" % t, p0, p1, t > 0)

        def rg(b):
            return [(b, c0, c1)]
        tt("xs", T.xs[:, c0:c1], T.IX[:, 0:n], T.BASE[:, 192 * t + c0:192 * t + c1], ALU.add, n,
           [("IX", 0, 1)] + base_rd, rg("xs"))
        ts("xu", T.xu[:, c0:c1], T.xs[:, c0:c1], 4095 - (1 << 31), None, ALU.bitwise_and, None, n, rg("xs"), rg("xu"))
        ts("xa", T.W[:, c0:c1], T.xu[:, c0:c1], 128.0, -0.03125, ALU.add, ALU.max, n, rg("xu"), [("W", 0, 1)] + rg("Wd"))
        tt("xq", T.xq[:, c0:c1], T.W[:, c0:c1], T.xu[:, c0:c1], ALU.mult, n, rg("xu") + [("W", 0, 1)] + rg("Wd"), rg("xq"))
        ts("xp", T.xp[:, c0:c1], T.xq[:, c0:c1], 7, 4095 | (3 << 18), ALU.logical_shift_right, ALU.bitwise_and, n,
           rg("xq"), rg("xp"))
        if t == 0:
            tt("xl", T.xp[:, c0:c1], T.E1[:, c0:c1], T.xp[:, c0:c1], ALU.max, n, rg("xp") + [("E1", 0, 1)], rg("xp"))
        ts("ix", T.IDX[:, c0:c1], T.xp[:, c0:c1], float(ZC), None, ALU.min, None, n, rg("xp"), rg("IDX"))

    def repeat(t, p):
        tb, tn, sn = TB[t % 2], "TB%d" % (t % 2), "S%d" % t
        c = 512 * o[p]
        b = next_bank()
        mm("rep", [(T[b][:, 64 * j:64 * j + 64], T.R[:, 128 * j:128 * j + 128], S[t][:, 64 * p:64 * p + 64],
                    True, True, 64) for j in range(8)],
           [("R", 0, 1024), (sn, 64 * p, 64 * p + 64)], [(b, 0, 1)])
        cp("ev", tb[:, c:c + 512], T[b][:], 512, [(b, 0, 1)], [(tn, c, c + 512)])

    for p in (7, 6, 0, 1, 2, 3):
        repeat(0, p)
    bs0 = spans(cfg["batch"][0])
    offsets(0, *bs0[0])
    for p in (4, 5):
        repeat(0, p)
    for b in bs0[1:]:
        offsets(0, *b)
    ts("lt", T.LT[:], T.E1[:, 0:192], 1.0, -16777216.0, ALU.min, ALU.mult, 192, [("E1", 0, 1)], [("LT", 0, 192)])
    for c0 in (0, 256):
        c1 = c0 + 256
        tt("bl", T.bl[:, c0:c1], S[0][:, c0:c1], T.lS[:, c0:c1], ALU.mult, 384, [("S0", c0, c1), ("lS", c0, c1)],
           [("bl", c0, c1)])
        ts("blb", T.bl[:, c0:c1], T.bl[:, c0:c1], -0.875, None, ALU.add, None, 128, [("bl", c0, c1)], [("bl", c0, c1)])

    def out_engines(p, p0, p1):
        ps = [x for x in range(p0, p1) if x < 6]
        if p == 6:
            return e_near[0:2] if ps else e_far
        n = len(e_far) // len(ps)
        return e_far[n * ps.index(p):n * ps.index(p) + n]

    eb = [0]
    sends = []
    for t in range(RO):
        ph[0] = t
        tb, tn = TB[t % 2], "TB%d" % (t % 2)
        gs = spans(cfg["gath"][t])
        done = [0]
        nxt = spans(cfg["batch"][t + 1]) if t + 1 < RO else []
        for (p0, p1) in spans(cfg["chunks"][t]):
            while done[0] < len(gs) and gs[done[0]][0] < p1:
                q0, q1 = gs[done[0]]
                done[0] += 1
                cp("ga", T.G[:, 384 * q0:384 * q1], tb[:, 0:TW].indirect(T.IDX[:, 24 * q0:24 * q1]), 0,
                   [(tn, 0, TW), ("IDX", 24 * q0, 24 * q1)], [("G", 384 * q0, 384 * q1)], gn=384 * (q1 - q0))
            g0, g1, c0, c1 = 384 * p0, 384 * p1, 64 * p0, 64 * p1
            n, w = g1 - g0, c1 - c0
            en = "E%d" % (eb[0] % 2)
            eb[0] += 1
            E = T[en][:, 0:w]
            mm("e1_", [(E, T.H[:], S[t][:, c0:c1], True, False, w), (E, T.H16[:], T.bl[:, c0:c1], False, False, w)]
               + [(E, T.P8[:], T.G[:, g0 + m:g1:6], False, False, w) for m in range(6)],
               [("H", 0, 128), ("H16", 0, 128), ("P8", 0, 128), ("S%d" % t, c0, c1), ("bl", c0, c1), ("G", g0, g1)],
               [(en, 0, 1)])
            V("mx", n / 2, [("DM", 0, nch), ("G", g0, g1)], [("MX", g0, g1)],
              lambda q, g0=g0, g1=g1, n=n: q.tensor_tensor_scan(T.MX[:, g0:g1], T.DM[:, 0:n], T.G[:, g0:g1], 0.0,
                                                                ALU.mult, ALU.max))
            V("mn", n / 2, [("DN", 0, nch), ("G", g0, g1)], [("MN", g0, g1)],
              lambda q, g0=g0, g1=g1, n=n: q.tensor_tensor_scan(T.MN[:, g0:g1], T.DN[:, 0:n], T.G[:, g0:g1], 0.0,
                                                                ALU.add, ALU.min))
            mm("e2_", [(E, T.N8[:], T.MX[:, g0 + 5:g1:6], False, False, w)], [("N8", 0, 128), ("MX", g0, g1)],
               [(en, 0, 1)])
            mm("e3_", [(E, T.N8[:], T.MN[:, g0 + 5:g1:6], False, True, w)], [("N8", 0, 128), ("MN", g0, g1)],
               [(en, 0, 1)])
            sn = "S%d" % (t + 1)
            ts("fl", S[t + 1][:, c0:c1], E, MAGIC, MAGIC, ALU.add, ALU.subtract, w, [(en, 0, 1)], [(sn, c0, c1)])
            if t + 1 < RO:
                for p in range(p0, p1):
                    repeat(t + 1, p)
                for (b0_, b1_) in nxt:
                    if p0 < b1_ <= p1:
                        offsets(t + 1, b0_, b1_)
            else:
                items = [(o[p], out_engines(p, p0, p1), "ayp" if p == 6 else "ayo", S[RO][:, 64 * p:64 * p + 64], T.Dy[r])
                         for p in range(p0, p1) if p < 7]
                if items:
                    sends.append((send("sy", items, [(sn, c0, min(c1, 448))]), p0, p1))

    last = spans(cfg["chunks"][RO - 1])
    n_far = sum(len(out_engines(p, p0, p1)) for (p0, p1) in last for p in range(p0, p1) if p < 6)
    n_near = sum(len(out_engines(6, p0, p1)) for (p0, p1) in last if p0 <= 6 < p1)
    s_far = [s for (s, p0, p1) in sends if p0 < 6][-1]
    s_near = [s for (s, p0, p1) in sends if p0 <= 6 < p1][0]
    ext("ayo", "ayo", n_far, 2600, [("Dyf", 0, 1)], after=[s_far])
    ext("ayp", "ayp", n_near, 2000, [("Dyn", 0, 1)], after=[s_near])
    runs = []
    for d in sorted(far):
        if runs and runs[-1][1] == d:
            runs[-1][1] = d + 1
        else:
            runs.append([d, d + 1])
    dma("yo", "a", "dy0", T.y[16 * r:16 * r + 16, :], S[RO][:, 448:512], [("S%d" % RO, 448, 512)], [])
    dmas("yf", "s", "dy2", [(T.y[16 * d0:16 * d1, :], T.Dy[d0:d1]) for d0, d1 in runs], [("Dyf", 0, 1)], [])
    dma("yn", "a", "dy1", T.y[16 * near:16 * near + 16, :], T.Dy[near], [("Dyn", 0, 1)], [])
    return ops, ["dy0", "dy1", "dy2"], loc[0]


def planned(ops):
    plan = {}
    for line in PLAN.strip().split("\n"):
        w = line.split()
        for a in w[1:]:
            k, v = a.split(":")
            plan[w[0] + k] = (int(v[:-1]), v[-1])
    n = len(ops)
    at = [plan[("s" if x["ph"] < 0 else "l" if x["ph"] == RO - 1 else "m") + x["key"]] for x in ops]
    when = [at[i][0] + PERIOD * max(ops[i]["ph"], 0) for i in range(n)]
    order, placed, rest = [], set(), set(range(n))
    while rest:
        i = min((when[k], k) for k in rest if all(d in placed for d in ops[k]["deps"]))[1]
        order.append(i)
        placed.add(i)
        rest.remove(i)
    return order, [a[1] for a in at]


def rank_program(g, core, T, topo):
    if T.rank_of(core) is None:
        return
    ops, fin, nloc = build(g, core, T, topo, CFG)
    order, eng = planned(ops)
    qs = {"p": g.tensor, "v": g.vector, "a": g.scalar, "g": g, "s": g.sync}
    count = {e: 0 for e in "pvag"}
    mark = [None] * len(ops)
    seen = {e: {} for e in qs}
    total = {}
    for i in order:
        op, e = ops[i], eng[i]
        if op["kind"] == "x":
            mark[i] = (op["sem"], op["val"])
            continue
        q = qs[e]
        need = {}
        for d, raw in op["deps"].items():
            if mark[d] is None or (ops[d]["kind"] == "c" and eng[d] == e and not raw):
                continue
            s, v = mark[d]
            need[s] = max(need.get(s, 0), v)
        for s, v in need.items():
            if seen[e].get(s, 0) < v:
                q.wait_ge(T.sem[s], v)
                seen[e][s] = v
        ins = op["emit"](q, e)
        if op["kind"] == "c":
            for x in ins:
                x.then_inc(T.sem["c_" + e], 1)
            count[e] += len(ins)
            mark[i] = ("c_" + e, count[e])
        elif op["kind"] == "d":
            for x in ins:
                x.then_inc(T.sem[op["sem"]], 16)
            total[op["sem"]] = total.get(op["sem"], 0) + 16 * len(ins)
            mark[i] = (op["sem"], total[op["sem"]])
    g.wait_ge(T.sem["loc"], nloc)
    for e in "pvag":
        g.wait_ge(T.sem["c_" + e], count[e])
    for s in fin:
        g.wait_ge(T.sem[s], total[s])
